import numpy as np, ml_dtypes
CORES = [23,119,17,113]
N = 4
VB, TK = 2, 64
def setup_inputs(rng):
    h = (rng.standard_normal((128, TK), dtype=np.float32) / 8).astype(ml_dtypes.bfloat16)
    return {"h": np.broadcast_to(h, (N, 128, TK)).copy(), "w": rng.standard_normal((N, 128, VB * 128), dtype=np.float32).astype(ml_dtypes.bfloat16)}
def setup_inputs_big(rng):
    d = setup_inputs(rng)
    for k in ("h", "w"): d[k] = (d[k].astype(np.float32) * 1024.0).astype(d[k].dtype)
    return d
def setup_inputs_small(rng):
    d = setup_inputs(rng)
    for k in ("h", "w"): d[k] = (d[k].astype(np.float32) * (1 / 1024.0)).astype(d[k].dtype)
    return d
def setup_inputs_apart(rng):
    d = setup_inputs(rng)
    f = (10.0 ** rng.permutation(np.linspace(-1.5, 1.5, N))).astype(np.float32).reshape(N, 1, 1)
    for k in ("w",): d[k] = (d[k].astype(np.float32) * f).astype(d[k].dtype)
    return d
def setup_inputs_neg(rng):
    d = setup_inputs(rng)
    d["h"] = (np.abs(d["h"].astype(np.float32)) * 1048576.0).astype(d["h"].dtype); d["w"] = (-np.abs(d["w"].astype(np.float32))).astype(d["w"].dtype)
    return d
def reference(h, w):
    H, W = h.astype(np.float64), w.astype(np.float64)
    Z = np.concatenate([W[r].T @ H[r] for r in range(N)], axis=0)
    m = Z.max(axis=0)
    s = np.maximum(Z - 0.5 * m, 0.0).sum(axis=0)
    return {"m": np.broadcast_to(m.astype(np.float32), (N, 1, TK)), "s": np.broadcast_to(s.astype(np.float32), (N, 1, TK))}

@@ -1,0 +1,156 @@
+from concourse.bass import DstId, RemoteDMATransfer
+from concourse.mybir import AluOpType
+
+N = 4
+TK = 64
+NE = 8
+OWN = 12
+
+SCRATCH = {
+    "h_sb": ("sbuf", [128, 64], "bfloat16"),
+    "w_sb": ("sbuf", [128, 256], "bfloat16"),
+    "shear": ("sbuf", [64, 65], "float32"),
+    "ident": ("sbuf", [64, 64], "float32"),
+    "flat": ("dram", [1, 64 * 65], "float32"),
+    "zeros": ("sbuf", [128, 64], "float32"),
+    "ones": ("sbuf", [128, 1], "float32"),
+    "nhalf": ("sbuf", [1, 128], "float32"),
+    "tree": ("sbuf", [64, 320], "float32"),
+    "xm": ("sbuf", [128, 16], "float32"),
+    "xs": ("sbuf", [128, 16], "float32"),
+    "cm": ("sbuf", [64, 4], "float32"),
+    "cs": ("sbuf", [64, 4], "float32"),
+    "mrow": ("sbuf", [1, 64], "float32"),
+    "relu": ("sbuf", [128, 128], "float32"),
+    "za0": ("psum", [128, 512], "float32"),
+    "za1": ("psum", [128, 512], "float32"),
+    "za2": ("psum", [128, 512], "float32"),
+    "za3": ("psum", [128, 512], "float32"),
+    "zb0": ("psum", [128, 512], "float32"),
+    "zb1": ("psum", [128, 512], "float32"),
+}
+SEMAPHORES = ["ld", "idf", "idr", "dv", "pa0", "pa1", "pa2", "pa3", "ptr", "pb0", "pb1", "psm",
+              "arr1", "arr2", "loc", "stm", "sts"]
+
+
+def _low_bits(mask, k):
+    out, bit = 0, 1
+    while k > 0:
+        if mask & bit:
+            out |= bit
+            k -= 1
+        bit <<= 1
+    return out
+
+
+def rank_program(g, core, T, topo):
+    rank = T.rank_of(core)
+    if rank is None:
+        return
+    S = T.sem
+    ve, pe = g.vector, g.tensor
+    others = sorted((c for c in T.cores if c != core), key=lambda c: topo.chip(c) == topo.chip(core))
+    for d in others:
+        assert topo.may_write(core, d)
+
+    def exchange(buf, sem):
+        allowed = topo.mask(core, others[0])
+        for d in others[1:]:
+            allowed &= topo.mask(core, d)
+        ids, dsts = [], []
+        for d in others:
+            rid, pid, _ = topo.addr(d)
+            slot = 4 * ((rank - T.rank_of(d) - 1) % N)
+            ids.append(DstId(rid=rid, pnc=pid))
+            dsts.append(buf[:, slot:slot + 1])
+        g.remote_dma_fused([RemoteDMATransfer(dst_ids=ids, dma_engine_mask=_low_bits(allowed, NE), remote_sem=sem,
+                                              srcs=[buf[:, OWN:OWN + 1]], dsts=dsts, alu_op=0)], local_sem=S.loc)
+
+    g.sync.dma_start(T.h_sb[:, :], T.h[:, :]).then_inc(S.ld, 16)
+    g.scalar.dma_start(T.w_sb[:, :], T.w[:, :]).then_inc(S.ld, 16)
+
+    n = [0]
+
+    def step(ins):
+        ins.then_inc(S.dv, 1)
+        n[0] += 1
+        ve.wait_ge(S.dv, n[0])
+        return n[0]
+
+    step(ve.memset(T.shear[:, 1:65], 0.0))
+    n_shear = step(ve.memset(T.shear[:, 0:1], 1.0))
+    step(ve.memset(T.xm[64:128, OWN:OWN + 4], 0.0))
+    step(ve.memset(T.xs[64:128, OWN:OWN + 4], 0.0))
+    step(ve.memset(T.nhalf[:, :], -0.5))
+    step(ve.memset(T.zeros[:, :], 0.0))
+    step(ve.memset(T.ones[:, :], 1.0))
+
+    g.sync.wait_ge(S.dv, n_shear)
+    g.sync.dma_start(T.flat[0, :], T.shear[:, :]).then_inc(S.idf, 16)
+    g.sync.wait_ge(S.idf, 16)
+    g.sync.dma_start(T.ident[:, :], T.flat[0, 0:64 * 64]).then_inc(S.idr, 16)
+
+    pe.wait_ge(S.ld, 32)
+    za = [T.za0, T.za1, T.za2, T.za3]
+    for j in range(4):
+        pe.matmul(za[j][0:64, 0:64], T.h_sb[:, :], T.w_sb[:, 64 * j:64 * j + 64], start=True, stop=True
+                  ).then_inc(S["pa%d" % j], 1)
+    zb = [T.zb0, T.zb1]
+    for b in range(2):
+        pe.matmul(zb[b][:, 0:64], T.w_sb[:, 128 * b:128 * b + 128], T.h_sb[:, :], start=True, stop=False)
+
+    tr = T.tree
+    ve.wait_ge(S.pa0, 1)
+    step(ve.tensor_copy(tr[:, 0:64], za[0][0:64, 0:64]))
+    for j in range(1, 4):
+        ve.wait_ge(S["pa%d" % j], 1)
+        step(ve.tensor_tensor(tr[:, 64 * j:64 * j + 64], za[j][0:64, 0:64], tr[:, 64 * j - 64:64 * j], AluOpType.max))
+    src, width = 192, 64
+    while width > 2:
+        half = width // 2
+        dst = src + width
+        step(ve.tensor_tensor(tr[:, dst:dst + half], tr[:, src:src + half], tr[:, src + half:src + width],
+                              AluOpType.max))
+        src, width = dst, half
+    n_loc = step(ve.tensor_tensor(T.xm[0:64, OWN:OWN + 1], tr[:, src:src + 1], tr[:, src + 1:src + 2], AluOpType.max))
+
+    g.wait_ge(S.dv, n_loc)
+    exchange(T.xm, S.arr1)
+
+    ve.wait_ge(S.arr1, 3 * NE)
+    step(ve.tensor_tensor(T.cm[:, 0:2], T.xm[0:64, 0:8:4], T.xm[0:64, 8:16:4], AluOpType.max))
+    n_m = step(ve.tensor_tensor(T.cm[:, 2:3], T.cm[:, 0:1], T.cm[:, 1:2], AluOpType.max))
+
+    pe.wait_ge(S.dv, n_m)
+    pe.wait_ge(S.idr, 16)
+    pe.matmul(T.za0[0:1, 0:64], T.cm[:, 2:3], T.ident[:, :], start=True, stop=True).then_inc(S.ptr, 1)
+    ve.wait_ge(S.ptr, 1)
+    n_row = step(ve.tensor_copy(T.mrow[:, :], T.za0[0:1, 0:64]))
+
+    g.sync.wait_ge(S.dv, n_row)
+    g.sync.dma_start(T.m[:, :], T.mrow[:, :]).then_inc(S.stm, 16)
+
+    pe.wait_ge(S.dv, n_row)
+    for b in range(2):
+        pe.matmul(zb[b][:, 0:64], T.nhalf[:, :], T.mrow[:, :], start=False, stop=True).then_inc(S["pb%d" % b], 1)
+    for b in range(2):
+        ve.wait_ge(S["pb%d" % b], 1)
+        n_r = step(ve.tensor_tensor(T.relu[:, 64 * b:64 * b + 64], zb[b][:, 0:64], T.zeros[:, :], AluOpType.max))
+        pe.wait_ge(S.dv, n_r)
+        mm = pe.matmul(T.za1[0:64, 0:1], T.relu[:, 64 * b:64 * b + 64], T.ones[:, :], start=(b == 0), stop=(b == 1))
+    mm.then_inc(S.psm, 1)
+    ve.wait_ge(S.psm, 1)
+    n_s = step(ve.tensor_copy(T.xs[0:64, OWN:OWN + 1], T.za1[0:64, 0:1]))
+
+    g.wait_ge(S.dv, n_s)
+    exchange(T.xs, S.arr2)
+
+    ve.wait_ge(S.arr2, 3 * NE)
+    step(ve.tensor_tensor(T.cs[:, 0:2], T.xs[0:64, 0:8:4], T.xs[0:64, 8:16:4], AluOpType.add))
+    n_end = step(ve.tensor_tensor(T.cs[:, 2:3], T.cs[:, 0:1], T.cs[:, 1:2], AluOpType.add))
+
+    g.scalar.wait_ge(S.dv, n_end)
+    g.scalar.dma_start(T.s[:, :], T.cs[:, 2:3]).then_inc(S.sts, 16)
+    g.scalar.wait_ge(S.sts, 16)
+    g.sync.wait_ge(S.stm, 16)
+    g.wait_ge(S.loc, 2 * NE)

@@ -1,5 +1,5 @@
 from concourse.bass import DstId, RemoteDMATransfer
-from concourse.mybir import AluOpType
+from concourse.mybir import AluOpType, AxisListType, ActivationFunctionType
 
 N = 4
 TK = 64
@@ -9,28 +9,15 @@ OWN = 12
 SCRATCH = {
     "h_sb": ("sbuf", [128, 64], "bfloat16"),
     "w_sb": ("sbuf", [128, 256], "bfloat16"),
-    "shear": ("sbuf", [64, 65], "float32"),
-    "ident": ("sbuf", [64, 64], "float32"),
-    "flat": ("dram", [1, 64 * 65], "float32"),
-    "zeros": ("sbuf", [128, 64], "float32"),
-    "ones": ("sbuf", [128, 1], "float32"),
-    "nhalf": ("sbuf", [1, 128], "float32"),
-    "tree": ("sbuf", [64, 320], "float32"),
     "xm": ("sbuf", [128, 16], "float32"),
     "xs": ("sbuf", [128, 16], "float32"),
     "cm": ("sbuf", [64, 4], "float32"),
+    "nb": ("sbuf", [64, 4], "float32"),
     "cs": ("sbuf", [64, 4], "float32"),
-    "mrow": ("sbuf", [1, 64], "float32"),
-    "relu": ("sbuf", [128, 128], "float32"),
-    "za0": ("psum", [128, 512], "float32"),
-    "za1": ("psum", [128, 512], "float32"),
-    "za2": ("psum", [128, 512], "float32"),
-    "za3": ("psum", [128, 512], "float32"),
-    "zb0": ("psum", [128, 512], "float32"),
-    "zb1": ("psum", [128, 512], "float32"),
+    "relu": ("sbuf", [64, 256], "float32"),
+    "z": ("psum", [128, 512], "float32"),
 }
-SEMAPHORES = ["ld", "idf", "idr", "dv", "pa0", "pa1", "pa2", "pa3", "ptr", "pb0", "pb1", "psm",
-              "arr1", "arr2", "loc", "stm", "sts"]
+SEMAPHORES = ["ld", "pz", "dv", "ac", "arr1", "arr2", "loc", "stm", "sts"]
 
 
 def _low_bits(mask, k):
@@ -48,7 +35,7 @@ def rank_program(g, core, T, topo):
     if rank is None:
         return
     S = T.sem
-    ve, pe = g.vector, g.tensor
+    ve, pe, act, sy = g.vector, g.tensor, g.scalar, g.sync
     others = sorted((c for c in T.cores if c != core), key=lambda c: topo.chip(c) == topo.chip(core))
     for d in others:
         assert topo.may_write(core, d)
@@ -66,9 +53,6 @@ def rank_program(g, core, T, topo):
         g.remote_dma_fused([RemoteDMATransfer(dst_ids=ids, dma_engine_mask=_low_bits(allowed, NE), remote_sem=sem,
                                               srcs=[buf[:, OWN:OWN + 1]], dsts=dsts, alu_op=0)], local_sem=S.loc)
 
-    g.sync.dma_start(T.h_sb[:, :], T.h[:, :]).then_inc(S.ld, 16)
-    g.scalar.dma_start(T.w_sb[:, :], T.w[:, :]).then_inc(S.ld, 16)
-
     n = [0]
 
     def step(ins):
@@ -77,80 +61,42 @@ def rank_program(g, core, T, topo):
         ve.wait_ge(S.dv, n[0])
         return n[0]
 
-    step(ve.memset(T.shear[:, 1:65], 0.0))
-    n_shear = step(ve.memset(T.shear[:, 0:1], 1.0))
+    sy.dma_start(T.h_sb[:, :], T.h[:, :]).then_inc(S.ld, 16)
+    act.dma_start(T.w_sb[:, :], T.w[:, :]).then_inc(S.ld, 16)
+
     step(ve.memset(T.xm[64:128, OWN:OWN + 4], 0.0))
     step(ve.memset(T.xs[64:128, OWN:OWN + 4], 0.0))
-    step(ve.memset(T.nhalf[:, :], -0.5))
-    step(ve.memset(T.zeros[:, :], 0.0))
-    step(ve.memset(T.ones[:, :], 1.0))
-
-    g.sync.wait_ge(S.dv, n_shear)
-    g.sync.dma_start(T.flat[0, :], T.shear[:, :]).then_inc(S.idf, 16)
-    g.sync.wait_ge(S.idf, 16)
-    g.sync.dma_start(T.ident[:, :], T.flat[0, 0:64 * 64]).then_inc(S.idr, 16)
 
     pe.wait_ge(S.ld, 32)
-    za = [T.za0, T.za1, T.za2, T.za3]
-    for j in range(4):
-        pe.matmul(za[j][0:64, 0:64], T.h_sb[:, :], T.w_sb[:, 64 * j:64 * j + 64], start=True, stop=True
-                  ).then_inc(S["pa%d" % j], 1)
-    zb = [T.zb0, T.zb1]
-    for b in range(2):
-        pe.matmul(zb[b][:, 0:64], T.w_sb[:, 128 * b:128 * b + 128], T.h_sb[:, :], start=True, stop=False)
-
-    tr = T.tree
-    ve.wait_ge(S.pa0, 1)
-    step(ve.tensor_copy(tr[:, 0:64], za[0][0:64, 0:64]))
-    for j in range(1, 4):
-        ve.wait_ge(S["pa%d" % j], 1)
-        step(ve.tensor_tensor(tr[:, 64 * j:64 * j + 64], za[j][0:64, 0:64], tr[:, 64 * j - 64:64 * j], AluOpType.max))
-    src, width = 192, 64
-    while width > 2:
-        half = width // 2
-        dst = src + width
-        step(ve.tensor_tensor(tr[:, dst:dst + half], tr[:, src:src + half], tr[:, src + half:src + width],
-                              AluOpType.max))
-        src, width = dst, half
-    n_loc = step(ve.tensor_tensor(T.xm[0:64, OWN:OWN + 1], tr[:, src:src + 1], tr[:, src + 1:src + 2], AluOpType.max))
+    pe.matmul(T.z[0:64, 0:256], T.h_sb[:, :], T.w_sb[:, :], start=True, stop=True).then_inc(S.pz, 1)
+    ve.wait_ge(S.pz, 1)
+    n_loc = step(ve.tensor_reduce(T.xm[0:64, OWN:OWN + 1], T.z[0:64, 0:256], AxisListType.X, AluOpType.max))
 
     g.wait_ge(S.dv, n_loc)
     exchange(T.xm, S.arr1)
 
     ve.wait_ge(S.arr1, 3 * NE)
     step(ve.tensor_tensor(T.cm[:, 0:2], T.xm[0:64, 0:8:4], T.xm[0:64, 8:16:4], AluOpType.max))
+    n_nb = step(ve.tensor_scalar(T.nb[:, 0:1], T.cm[:, 0:1], T.cm[:, 1:2], -0.5, AluOpType.max, AluOpType.mult))
+
+    act.wait_ge(S.dv, n_nb)
+    act.activation(T.relu[:, :], T.z[0:64, 0:256], ActivationFunctionType.Relu, bias=T.nb[:, 0:1], scale=1.0,
+                   accum_out=T.xs[0:64, OWN:OWN + 1]).then_inc(S.ac, 1)
+
     n_m = step(ve.tensor_tensor(T.cm[:, 2:3], T.cm[:, 0:1], T.cm[:, 1:2], AluOpType.max))
+    sy.wait_ge(S.dv, n_m)
+    sy.dma_start(T.m[:, :], T.cm[:, 2:3]).then_inc(S.stm, 16)
 
-    pe.wait_ge(S.dv, n_m)
-    pe.wait_ge(S.idr, 16)
-    pe.matmul(T.za0[0:1, 0:64], T.cm[:, 2:3], T.ident[:, :], start=True, stop=True).then_inc(S.ptr, 1)
-    ve.wait_ge(S.ptr, 1)
-    n_row = step(ve.tensor_copy(T.mrow[:, :], T.za0[0:1, 0:64]))
-
-    g.sync.wait_ge(S.dv, n_row)
-    g.sync.dma_start(T.m[:, :], T.mrow[:, :]).then_inc(S.stm, 16)
-
-    pe.wait_ge(S.dv, n_row)
-    for b in range(2):
-        pe.matmul(zb[b][:, 0:64], T.nhalf[:, :], T.mrow[:, :], start=False, stop=True).then_inc(S["pb%d" % b], 1)
-    for b in range(2):
-        ve.wait_ge(S["pb%d" % b], 1)
-        n_r = step(ve.tensor_tensor(T.relu[:, 64 * b:64 * b + 64], zb[b][:, 0:64], T.zeros[:, :], AluOpType.max))
-        pe.wait_ge(S.dv, n_r)
-        mm = pe.matmul(T.za1[0:64, 0:1], T.relu[:, 64 * b:64 * b + 64], T.ones[:, :], start=(b == 0), stop=(b == 1))
-    mm.then_inc(S.psm, 1)
-    ve.wait_ge(S.psm, 1)
-    n_s = step(ve.tensor_copy(T.xs[0:64, OWN:OWN + 1], T.za1[0:64, 0:1]))
-
-    g.wait_ge(S.dv, n_s)
+    g.wait_ge(S.ac, 1)
     exchange(T.xs, S.arr2)
 
+    ve.wait_ge(S.ac, 1)
     ve.wait_ge(S.arr2, 3 * NE)
     step(ve.tensor_tensor(T.cs[:, 0:2], T.xs[0:64, 0:8:4], T.xs[0:64, 8:16:4], AluOpType.add))
     n_end = step(ve.tensor_tensor(T.cs[:, 2:3], T.cs[:, 0:1], T.cs[:, 1:2], AluOpType.add))
 
-    g.scalar.wait_ge(S.dv, n_end)
-    g.scalar.dma_start(T.s[:, :], T.cs[:, 2:3]).then_inc(S.sts, 16)
-    g.scalar.wait_ge(S.sts, 16)
-    g.sync.wait_ge(S.stm, 16)
+    act.wait_ge(S.dv, n_end)
+    act.dma_start(T.s[:, :], T.cs[:, 2:3]).then_inc(S.sts, 16)
+    act.wait_ge(S.sts, 16)
+    sy.wait_ge(S.stm, 16)
     g.wait_ge(S.loc, 2 * NE)

@@ -11,13 +11,14 @@ SCRATCH = {
     "w_sb": ("sbuf", [128, 256], "bfloat16"),
     "xm": ("sbuf", [128, 16], "float32"),
     "xs": ("sbuf", [128, 16], "float32"),
+    "nm": ("sbuf", [64, 4], "float32"),
     "cm": ("sbuf", [64, 4], "float32"),
-    "nb": ("sbuf", [64, 4], "float32"),
+    "hs": ("sbuf", [64, 4], "float32"),
     "cs": ("sbuf", [64, 4], "float32"),
     "relu": ("sbuf", [64, 256], "float32"),
     "z": ("psum", [128, 512], "float32"),
 }
-SEMAPHORES = ["ld", "pz", "dv", "ac", "arr1", "arr2", "loc", "stm", "sts"]
+SEMAPHORES = ["ld", "pz", "dv", "ac", "fin", "arr1", "arr2", "loc", "stm", "sts"]
 
 
 def _low_bits(mask, k):
@@ -70,33 +71,32 @@ def rank_program(g, core, T, topo):
     pe.wait_ge(S.ld, 32)
     pe.matmul(T.z[0:64, 0:256], T.h_sb[:, :], T.w_sb[:, :], start=True, stop=True).then_inc(S.pz, 1)
     ve.wait_ge(S.pz, 1)
-    n_loc = step(ve.tensor_reduce(T.xm[0:64, OWN:OWN + 1], T.z[0:64, 0:256], AxisListType.X, AluOpType.max))
+    n_loc = step(ve.tensor_reduce(T.xm[0:64, OWN:OWN + 1], T.z[0:64, 0:256], AxisListType.X, AluOpType.max,
+                                  negate=True))
 
     g.wait_ge(S.dv, n_loc)
     exchange(T.xm, S.arr1)
 
     ve.wait_ge(S.arr1, 3 * NE)
-    step(ve.tensor_tensor(T.cm[:, 0:2], T.xm[0:64, 0:8:4], T.xm[0:64, 8:16:4], AluOpType.max))
-    n_nb = step(ve.tensor_scalar(T.nb[:, 0:1], T.cm[:, 0:1], T.cm[:, 1:2], -0.5, AluOpType.max, AluOpType.mult))
+    n_nm = step(ve.tensor_reduce(T.nm[:, 0:1], T.xm[0:64, 0:16:4], AxisListType.X, AluOpType.min))
 
-    act.wait_ge(S.dv, n_nb)
-    act.activation(T.relu[:, :], T.z[0:64, 0:256], ActivationFunctionType.Relu, bias=T.nb[:, 0:1], scale=1.0,
+    act.wait_ge(S.dv, n_nm)
+    act.activation(T.relu[:, :], T.z[0:64, 0:256], ActivationFunctionType.Relu, bias=T.nm[:, 0:1], scale=2.0,
                    accum_out=T.xs[0:64, OWN:OWN + 1]).then_inc(S.ac, 1)
 
-    n_m = step(ve.tensor_tensor(T.cm[:, 2:3], T.cm[:, 0:1], T.cm[:, 1:2], AluOpType.max))
+    n_m = step(ve.tensor_scalar(T.cm[:, 0:1], T.nm[:, 0:1], -1.0, None, AluOpType.mult))
     sy.wait_ge(S.dv, n_m)
-    sy.dma_start(T.m[:, :], T.cm[:, 2:3]).then_inc(S.stm, 16)
+    sy.dma_start(T.m[:, :], T.cm[:, 0:1]).then_inc(S.stm, 16)
 
     g.wait_ge(S.ac, 1)
     exchange(T.xs, S.arr2)
 
-    ve.wait_ge(S.ac, 1)
-    ve.wait_ge(S.arr2, 3 * NE)
-    step(ve.tensor_tensor(T.cs[:, 0:2], T.xs[0:64, 0:8:4], T.xs[0:64, 8:16:4], AluOpType.add))
-    n_end = step(ve.tensor_tensor(T.cs[:, 2:3], T.cs[:, 0:1], T.cs[:, 1:2], AluOpType.add))
-
-    act.wait_ge(S.dv, n_end)
-    act.dma_start(T.s[:, :], T.cs[:, 2:3]).then_inc(S.sts, 16)
+    act.wait_ge(S.ac, 1)
+    act.wait_ge(S.arr2, 3 * NE)
+    act.activation(T.hs[:, 0:4], T.xs[0:64, 0:16:4], ActivationFunctionType.Identity, scale=0.5,
+                   accum_out=T.cs[:, 0:1]).then_inc(S.fin, 1)
+    act.wait_ge(S.fin, 1)
+    act.dma_start(T.s[:, :], T.cs[:, 0:1]).then_inc(S.sts, 16)
     act.wait_ge(S.sts, 16)
     sy.wait_ge(S.stm, 16)
     g.wait_ge(S.loc, 2 * NE)

@@ -3,22 +3,24 @@ from concourse.mybir import AluOpType, AxisListType, ActivationFunctionType
 
 N = 4
 TK = 64
+V = 256
 NE = 8
-OWN = 12
+BANK = 512
 
 SCRATCH = {
-    "h_sb": ("sbuf", [128, 64], "bfloat16"),
-    "w_sb": ("sbuf", [128, 256], "bfloat16"),
+    "h_sb": ("sbuf", [128, TK], "bfloat16"),
+    "w_sb": ("sbuf", [128, V], "bfloat16"),
+    "wp": ("sbuf", [128, V], "bfloat16"),
     "xm": ("sbuf", [128, 16], "float32"),
-    "xs": ("sbuf", [128, 16], "float32"),
+    "xs": ("sbuf", [128, 8], "float32"),
     "nm": ("sbuf", [64, 4], "float32"),
     "cm": ("sbuf", [64, 4], "float32"),
-    "hs": ("sbuf", [64, 4], "float32"),
+    "hs": ("sbuf", [64, 8], "float32"),
     "cs": ("sbuf", [64, 4], "float32"),
-    "relu": ("sbuf", [64, 256], "float32"),
-    "z": ("psum", [128, 512], "float32"),
+    "relu": ("sbuf", [64, 2 * V], "float32"),
+    "z": ("psum", [128, 2 * BANK], "float32"),
 }
-SEMAPHORES = ["ld", "pz", "dv", "ac", "fin", "arr1", "arr2", "loc", "stm", "sts"]
+SEMAPHORES = ["ldw", "ldh", "pz", "dv", "ac", "fin", "arrw", "arr1", "arr2", "loc", "stm", "sts"]
 
 
 def _low_bits(mask, k):
@@ -37,22 +39,23 @@ def rank_program(g, core, T, topo):
         return
     S = T.sem
     ve, pe, act, sy = g.vector, g.tensor, g.scalar, g.sync
-    others = sorted((c for c in T.cores if c != core), key=lambda c: topo.chip(c) == topo.chip(core))
-    for d in others:
-        assert topo.may_write(core, d)
+    near = [c for c in T.cores if c != core and topo.chip(c) == topo.chip(core)]
+    far = sorted((c for c in T.cores if topo.chip(c) != topo.chip(core)), key=lambda c: topo.die(c) != topo.die(core))
+    assert len(near) == 1 and len(far) == 2 and topo.die(far[0]) == topo.die(core) != topo.die(far[1])
+    allowed = None
+    for c in near + far:
+        assert topo.may_write(core, c)
+        allowed = topo.mask(core, c) if allowed is None else allowed & topo.mask(core, c)
+    engines = _low_bits(allowed, NE)
+    chip_only = _low_bits(topo.mask(core, near[0]) & ~allowed, NE)
 
-    def exchange(buf, sem):
-        allowed = topo.mask(core, others[0])
-        for d in others[1:]:
-            allowed &= topo.mask(core, d)
-        ids, dsts = [], []
-        for d in others:
-            rid, pid, _ = topo.addr(d)
-            slot = 4 * ((rank - T.rank_of(d) - 1) % N)
+    def send(src, pairs, sem, eng):
+        ids = []
+        for c, _ in pairs:
+            rid, pid, _se = topo.addr(c)
             ids.append(DstId(rid=rid, pnc=pid))
-            dsts.append(buf[:, slot:slot + 1])
-        g.remote_dma_fused([RemoteDMATransfer(dst_ids=ids, dma_engine_mask=_low_bits(allowed, NE), remote_sem=sem,
-                                              srcs=[buf[:, OWN:OWN + 1]], dsts=dsts, alu_op=0)], local_sem=S.loc)
+        g.remote_dma_fused([RemoteDMATransfer(dst_ids=ids, dma_engine_mask=eng, remote_sem=sem, srcs=[src],
+                                              dsts=[ap for _, ap in pairs], alu_op=0)], local_sem=S.loc)
 
     n = [0]
 
@@ -62,41 +65,50 @@ def rank_program(g, core, T, topo):
         ve.wait_ge(S.dv, n[0])
         return n[0]
 
-    sy.dma_start(T.h_sb[:, :], T.h[:, :]).then_inc(S.ld, 16)
-    act.dma_start(T.w_sb[:, :], T.w[:, :]).then_inc(S.ld, 16)
+    sy.dma_start(T.w_sb[:, :], T.w[:, :]).then_inc(S.ldw, 16)
+    act.dma_start(T.h_sb[:, :], T.h[:, :]).then_inc(S.ldh, 16)
 
-    step(ve.memset(T.xm[64:128, OWN:OWN + 4], 0.0))
-    step(ve.memset(T.xs[64:128, OWN:OWN + 4], 0.0))
+    g.wait_ge(S.ldw, 16)
+    send(T.w_sb[:, :], [(near[0], T.wp[:, :])], S.arrw, chip_only)
 
-    pe.wait_ge(S.ld, 32)
-    pe.matmul(T.z[0:64, 0:256], T.h_sb[:, :], T.w_sb[:, :], start=True, stop=True).then_inc(S.pz, 1)
+    step(ve.memset(T.xm[64:128, 12:16], 0.0))
+    step(ve.memset(T.xs[:, 4:8], 0.0))
+
+    pe.wait_ge(S.ldw, 16)
+    pe.wait_ge(S.ldh, 16)
+    pe.matmul(T.z[0:64, 0:V], T.h_sb[:, :], T.w_sb[:, :], start=True, stop=True).then_inc(S.pz, 1)
     ve.wait_ge(S.pz, 1)
-    n_loc = step(ve.tensor_reduce(T.xm[0:64, OWN:OWN + 1], T.z[0:64, 0:256], AxisListType.X, AluOpType.max,
-                                  negate=True))
+    n_loc = step(ve.tensor_reduce(T.xm[0:64, 12:13], T.z[0:64, 0:V], AxisListType.X, AluOpType.max, negate=True))
 
     g.wait_ge(S.dv, n_loc)
-    exchange(T.xm, S.arr1)
+    send(T.xm[:, 12:13], [(far[0], T.xm[:, 0:1]), (far[1], T.xm[:, 4:5]), (near[0], T.xm[:, 8:9])], S.arr1, engines)
+
+    pe.wait_ge(S.arrw, NE)
+    pe.matmul(T.z[0:64, BANK:BANK + V], T.h_sb[:, :], T.wp[:, :], start=True, stop=True).then_inc(S.pz, 1)
 
     ve.wait_ge(S.arr1, 3 * NE)
     n_nm = step(ve.tensor_reduce(T.nm[:, 0:1], T.xm[0:64, 0:16:4], AxisListType.X, AluOpType.min))
 
     act.wait_ge(S.dv, n_nm)
-    act.activation(T.relu[:, :], T.z[0:64, 0:256], ActivationFunctionType.Relu, bias=T.nm[:, 0:1], scale=2.0,
-                   accum_out=T.xs[0:64, OWN:OWN + 1]).then_inc(S.ac, 1)
+    act.activation(T.relu[:, 0:V], T.z[0:64, 0:V], ActivationFunctionType.Relu, bias=T.nm[:, 0:1], scale=2.0,
+                   accum_out=T.xs[0:64, 4:5]).then_inc(S.ac, 1)
+    act.wait_ge(S.pz, 2)
+    act.activation(T.relu[:, V:2 * V], T.z[0:64, BANK:BANK + V], ActivationFunctionType.Relu, bias=T.nm[:, 0:1],
+                   scale=2.0, accum_out=T.xs[0:64, 5:6]).then_inc(S.ac, 1)
 
     n_m = step(ve.tensor_scalar(T.cm[:, 0:1], T.nm[:, 0:1], -1.0, None, AluOpType.mult))
     sy.wait_ge(S.dv, n_m)
     sy.dma_start(T.m[:, :], T.cm[:, 0:1]).then_inc(S.stm, 16)
 
-    g.wait_ge(S.ac, 1)
-    exchange(T.xs, S.arr2)
+    g.wait_ge(S.ac, 2)
+    send(T.xs[:, 4:8], [(far[0], T.xs[:, 0:4])], S.arr2, engines)
 
-    act.wait_ge(S.ac, 1)
-    act.wait_ge(S.arr2, 3 * NE)
-    act.activation(T.hs[:, 0:4], T.xs[0:64, 0:16:4], ActivationFunctionType.Identity, scale=0.5,
+    act.wait_ge(S.ac, 2)
+    act.wait_ge(S.arr2, NE)
+    act.activation(T.hs[:, 0:8], T.xs[0:64, 0:8], ActivationFunctionType.Identity, scale=0.5,
                    accum_out=T.cs[:, 0:1]).then_inc(S.fin, 1)
     act.wait_ge(S.fin, 1)
     act.dma_start(T.s[:, :], T.cs[:, 0:1]).then_inc(S.sts, 16)
     act.wait_ge(S.sts, 16)
     sy.wait_ge(S.stm, 16)
-    g.wait_ge(S.loc, 2 * NE)
+    g.wait_ge(S.loc, 3 * NE)

from concourse.bass import DstId, RemoteDMATransfer
from concourse.mybir import AluOpType, AxisListType, ActivationFunctionType

N = 4
TK = 64
V = 256
NE = 8
BANK = 512

SCRATCH = {
    "h_sb": ("sbuf", [128, TK], "bfloat16"),
    "w_sb": ("sbuf", [128, V], "bfloat16"),
    "wp": ("sbuf", [128, V], "bfloat16"),
    "xm": ("sbuf", [128, 16], "float32"),
    "xs": ("sbuf", [128, 8], "float32"),
    "nm": ("sbuf", [64, 4], "float32"),
    "cm": ("sbuf", [64, 4], "float32"),
    "hs": ("sbuf", [64, 8], "float32"),
    "cs": ("sbuf", [64, 4], "float32"),
    "relu": ("sbuf", [64, 2 * V], "float32"),
    "z": ("psum", [128, 2 * BANK], "float32"),
}
SEMAPHORES = ["ldw", "ldh", "pz", "dv", "ac", "fin", "arrw", "arr1", "arr2", "loc", "stm", "sts"]


def _low_bits(mask, k):
    out, bit = 0, 1
    while k > 0:
        if mask & bit:
            out |= bit
            k -= 1
        bit <<= 1
    return out


def rank_program(g, core, T, topo):
    rank = T.rank_of(core)
    if rank is None:
        return
    S = T.sem
    ve, pe, act, sy = g.vector, g.tensor, g.scalar, g.sync
    near = [c for c in T.cores if c != core and topo.chip(c) == topo.chip(core)]
    far = sorted((c for c in T.cores if topo.chip(c) != topo.chip(core)), key=lambda c: topo.die(c) != topo.die(core))
    assert len(near) == 1 and len(far) == 2 and topo.die(far[0]) == topo.die(core) != topo.die(far[1])
    allowed = None
    for c in near + far:
        assert topo.may_write(core, c)
        allowed = topo.mask(core, c) if allowed is None else allowed & topo.mask(core, c)
    engines = _low_bits(allowed, NE)
    chip_only = _low_bits(topo.mask(core, near[0]) & ~allowed, NE)

    def send(src, pairs, sem, eng):
        ids = []
        for c, _ in pairs:
            rid, pid, _se = topo.addr(c)
            ids.append(DstId(rid=rid, pnc=pid))
        g.remote_dma_fused([RemoteDMATransfer(dst_ids=ids, dma_engine_mask=eng, remote_sem=sem, srcs=[src],
                                              dsts=[ap for _, ap in pairs], alu_op=0)], local_sem=S.loc)

    n = [0]

    def step(ins):
        ins.then_inc(S.dv, 1)
        n[0] += 1
        ve.wait_ge(S.dv, n[0])
        return n[0]

    sy.dma_start(T.w_sb[:, :], T.w[:, :]).then_inc(S.ldw, 16)
    act.dma_start(T.h_sb[:, :], T.h[:, :]).then_inc(S.ldh, 16)

    g.wait_ge(S.ldw, 16)
    send(T.w_sb[:, :], [(near[0], T.wp[:, :])], S.arrw, chip_only)

    step(ve.memset(T.xm[64:128, 12:16], 0.0))
    step(ve.memset(T.xs[:, 4:8], 0.0))

    pe.wait_ge(S.ldw, 16)
    pe.wait_ge(S.ldh, 16)
    pe.matmul(T.z[0:64, 0:V], T.h_sb[:, :], T.w_sb[:, :], start=True, stop=True).then_inc(S.pz, 1)
    ve.wait_ge(S.pz, 1)
    n_loc = step(ve.tensor_reduce(T.xm[0:64, 12:13], T.z[0:64, 0:V], AxisListType.X, AluOpType.max, negate=True))

    g.wait_ge(S.dv, n_loc)
    send(T.xm[:, 12:13], [(far[0], T.xm[:, 0:1]), (far[1], T.xm[:, 4:5]), (near[0], T.xm[:, 8:9])], S.arr1, engines)

    pe.wait_ge(S.arrw, NE)
    pe.matmul(T.z[0:64, BANK:BANK + V], T.h_sb[:, :], T.wp[:, :], start=True, stop=True).then_inc(S.pz, 1)

    ve.wait_ge(S.arr1, 3 * NE)
    n_nm = step(ve.tensor_reduce(T.nm[:, 0:1], T.xm[0:64, 0:16:4], AxisListType.X, AluOpType.min))

    act.wait_ge(S.dv, n_nm)
    act.activation(T.relu[:, 0:V], T.z[0:64, 0:V], ActivationFunctionType.Relu, bias=T.nm[:, 0:1], scale=2.0,
                   accum_out=T.xs[0:64, 4:5]).then_inc(S.ac, 1)
    act.wait_ge(S.pz, 2)
    act.activation(T.relu[:, V:2 * V], T.z[0:64, BANK:BANK + V], ActivationFunctionType.Relu, bias=T.nm[:, 0:1],
                   scale=2.0, accum_out=T.xs[0:64, 5:6]).then_inc(S.ac, 1)

    n_m = step(ve.tensor_scalar(T.cm[:, 0:1], T.nm[:, 0:1], -1.0, None, AluOpType.mult))
    sy.wait_ge(S.dv, n_m)
    sy.dma_start(T.m[:, :], T.cm[:, 0:1]).then_inc(S.stm, 16)

    g.wait_ge(S.ac, 2)
    send(T.xs[:, 4:8], [(far[0], T.xs[:, 0:4])], S.arr2, engines)

    act.wait_ge(S.ac, 2)
    act.wait_ge(S.arr2, NE)
    act.activation(T.hs[:, 0:8], T.xs[0:64, 0:8], ActivationFunctionType.Identity, scale=0.5,
                   accum_out=T.cs[:, 0:1]).then_inc(S.fin, 1)
    act.wait_ge(S.fin, 1)
    act.dma_start(T.s[:, :], T.cs[:, 0:1]).then_inc(S.sts, 16)
    act.wait_ge(S.sts, 16)
    sy.wait_ge(S.stm, 16)
    g.wait_ge(S.loc, 3 * NE)
